import numpy as np
import ml_dtypes


def mxq(x, axis, fmt="e4m3"):
    dtype, down = {"e4m3": (ml_dtypes.float8_e4m3fn, 7), "e5m2": (ml_dtypes.float8_e5m2, 14)}[fmt]
    v = np.moveaxis(np.asarray(x, np.float32).astype(ml_dtypes.bfloat16).astype(np.float64), axis, -1)
    blocks = v.reshape(v.shape[:-1] + (-1, 32))
    amax = np.abs(blocks).max(-1, keepdims=True)
    byte = np.maximum(np.where(amax > 0, np.frexp(amax)[1] - 1 + 127, 0) - down, 1)
    scale = np.exp2(byte - 127.0)
    codes = (blocks / scale).astype(np.float32).astype(dtype).astype(np.float64)
    return np.moveaxis((codes * scale).reshape(v.shape), -1, axis)


WIDE = False


def mx_kscale(k):
    if not WIDE:
        return np.ones(k)
    levels = np.array([10, -10, 5, -5, 0])
    if k % 512:
        return np.exp2(np.random.permutation(np.resize(levels, k // 32))).repeat(32)
    a = np.empty((k // 512, 16))
    for p in range(k // 512):
        a[p, :8] = np.random.permutation(np.resize(levels, 8))
        for g in range(8):
            far = levels[np.abs(levels - a[p, g]) >= 10]
            a[p, g + 8] = far[np.random.randint(len(far))]
    return np.exp2(a.ravel()).repeat(32)


def f64(x):
    return np.asarray(x).astype(np.float64)


def striped(idx):
    return np.tile(idx.reshape(-1, 16).T, (8, 1)).astype(np.uint16)


def unstriped(offs):
    return offs[:16].T.reshape(-1).astype(np.int64)


K, T, D, S, V, N = 1536, 1024, 2, 768, 384, 256


def setup_inputs():
    n = np.random.standard_normal
    s = mx_kscale(K)[:, None]
    return {
        "xT": (n((K, T)) * s).astype(np.float32),
        "w": (n((D, K, N)) / np.sqrt(D * K) / s[None]).astype(np.float32),
        "b": (0.3 * n((N, 1))).astype(np.float32),
        "offs": striped(np.random.permutation(T)[:S]),
    }


def reference(xT, w, b, offs):
    idx = unstriped(offs)
    xq = mxq(f64(xT)[:, idx], 0, "e4m3")
    wq = mxq(f64(w), 1, "e4m3")
    y = sum(wq[d].T @ xq[:, d * V:(d + 1) * V] for d in range(D))
    y = y + f64(b)
    return y

@@ -1,0 +1,193 @@
+from contextlib import ExitStack
+
+import concourse.mybir as mybir
+
+K, T, D, S, V, N = 1536, 1024, 2, 768, 384, 256
+FLOPS = 2 * N * V * D * K
+
+F32 = mybir.dt.float32
+BF16 = mybir.dt.bfloat16
+U32 = mybir.dt.uint32
+U16 = mybir.dt.uint16
+U8 = mybir.dt.uint8
+FP8X4 = mybir.dt.float8_e4m3fn_x4
+COPY = mybir.ActivationFunctionType.Copy
+IDENTITY = mybir.ActivationFunctionType.Identity
+ADD = mybir.AluOpType.add
+
+P = 128
+PACK = 4
+K_PASS = P * PACK
+PASSES = K // K_PASS
+HALF = 512
+X_SCALAR = {(0, 0): 176, (0, 1): 176, (1, 0): 384, (1, 1): 320, (2, 0): 352, (2, 1): 192}
+W_SCALAR = {(0, 0): 256, (0, 1): 256, (1, 0): 256, (1, 1): 256, (2, 0): 256, (2, 1): 128}
+M_TILES = N // P
+PIECES = ((0, 256), (256, 384))
+
+
+def regroup(dst, raw):
+    return (
+        dst.rearrange("p (c i) t -> p c t i", i=4),
+        raw.rearrange("p t (c i) -> p c t i", i=4),
+    )
+
+
+def tile_picked_merge_lin_bias_sub_e_kernel(tc, xT, w, b, offs, out):
+    nc = tc.nc
+    with ExitStack() as ctx:
+        keep = ctx.enter_context(tc.tile_pool(name="keep", bufs=1))
+        psum = ctx.enter_context(tc.psum_pool(name="psum", bufs=1))
+
+        offsets = keep.tile([P, S // 16], U16, name="offsets")
+        bias = keep.tile([P, M_TILES, 1], F32, name="bias")
+        warm = keep.tile([P, 1], F32, name="warm")
+        warmed = keep.tile([P, 1], F32, name="warmed")
+        nc.gpsimd.memset(warm[:], 0.0)
+        nc.scalar.activation(out=warmed[:], in_=warm[:], func=IDENTITY)
+
+        x_scales = keep.tile([P, T], U8, name="x_scales", align_bytes=64)
+        nc.gpsimd.memset(x_scales[:], 0)
+
+        x_raw = {}
+        w_raw = {}
+
+        def load_x(c, h):
+            x_raw[c, h] = keep.tile([P, PACK, HALF], F32, name=f"x_raw_{c}_{h}")
+            rows = xT[c * K_PASS : (c + 1) * K_PASS, h * HALF : (h + 1) * HALF]
+            nc.sync.dma_start(out=x_raw[c, h][:], in_=rows.rearrange("(p j) w -> p j w", j=PACK))
+
+        def load_w(c, d):
+            w_raw[c, d] = keep.tile([P, PACK, N], F32, name=f"w_raw_{c}_{d}")
+            rows = w[d, c * K_PASS : (c + 1) * K_PASS, :]
+            nc.sync.dma_start(out=w_raw[c, d][:], in_=rows.rearrange("(p j) n -> p j n", j=PACK))
+
+        load_x(0, 0)
+        nc.sync.dma_start(offsets[:], offs)
+        nc.scalar.dma_start(out=bias[:], in_=b.rearrange("(c p) o -> p c o", p=P))
+        load_x(0, 1)
+        load_x(1, 0)
+        load_x(1, 1)
+        load_x(2, 0)
+        load_w(0, 0)
+        load_x(2, 1)
+        load_w(0, 1)
+        for c in (1, 2):
+            for d in range(D):
+                load_w(c, d)
+
+        x_bf = {}
+        for c in range(PASSES):
+            for h in range(2):
+                x_bf[c, h] = keep.tile([P, HALF, PACK], BF16, name=f"x_bf_{c}_{h}", align_bytes=64)
+        x_codes = [keep.tile([P, T], U32, name=f"x_codes_{c}", align_bytes=64) for c in range(PASSES)]
+        g_codes = [keep.tile([P, S], U32, name=f"g_codes_{c}", align_bytes=64) for c in range(PASSES)]
+        g_scales = keep.tile([P, S], U8, name="g_scales", align_bytes=64)
+
+        w_bf = {}
+        w_codes = {}
+        w_scales = {}
+        for c in range(PASSES):
+            for d in range(D):
+                w_bf[c, d] = keep.tile([P, N, PACK], BF16, name=f"w_bf_{c}_{d}", align_bytes=64)
+                w_codes[c, d] = keep.tile([P, N], U32, name=f"w_codes_{c}_{d}", align_bytes=64)
+                w_scales[c, d] = keep.tile([P, N], U8, name=f"w_scales_{c}_{d}", align_bytes=64)
+
+        def cast(dst, raw, cut, width):
+            if cut > 0:
+                out_view, in_view = regroup(dst[:, :cut, :], raw[:, :, :cut])
+                nc.scalar.activation(out=out_view, in_=in_view, func=COPY)
+            if cut < width:
+                out_view, in_view = regroup(dst[:, cut:, :], raw[:, :, cut:])
+                nc.vector.tensor_copy(out=out_view, in_=in_view)
+
+        def cast_x(c, h):
+            cast(x_bf[c, h], x_raw[c, h], X_SCALAR[c, h], HALF)
+
+        def cast_w(c, d):
+            cast(w_bf[c, d], w_raw[c, d], W_SCALAR[c, d], N)
+
+        def quantize_x(c, h):
+            cols = slice(h * HALF, (h + 1) * HALF)
+            nc.vector.quantize_mx(
+                out=x_codes[c][:, cols].bitcast(FP8X4),
+                scales=x_scales[4 * c : P, cols],
+                in_=x_bf[c, h][:].rearrange("p w j -> p (w j)"),
+            )
+
+        def gather_codes(c):
+            nc.vector.tensor_copy(out=g_codes[c][:], in_=x_codes[c][:].indirect(offsets[:]))
+
+        def quantize_w(c, d, m0=0, m1=N):
+            nc.vector.quantize_mx(
+                out=w_codes[c, d][:, m0:m1].bitcast(FP8X4),
+                scales=w_scales[c, d][:, m0:m1],
+                in_=w_bf[c, d][:, m0:m1, :].rearrange("p n j -> p (n j)"),
+            )
+
+        def gather_scales():
+            nc.vector.tensor_copy(out=g_scales[:], in_=x_scales[:].indirect(offsets[:]))
+
+        acc = {}
+        for m in range(M_TILES):
+            for i, (v0, v1) in enumerate(PIECES):
+                acc[m, i] = psum.tile([P, v1 - v0], F32, name=f"acc_{m}_{i}")
+
+        def multiply(c, d):
+            for m in (1, 0):
+                m_cols = slice(m * P, (m + 1) * P)
+                for i, (v0, v1) in enumerate(PIECES):
+                    v_cols = slice(d * V + v0, d * V + v1)
+                    nc.tensor.matmul_mx(
+                        out=acc[m, i][:],
+                        lhsT=w_codes[c, d][:, m_cols].bitcast(FP8X4),
+                        lhsT_scale=w_scales[c, d][:, m_cols],
+                        rhs=g_codes[c][:, v_cols].bitcast(FP8X4),
+                        rhs_scale=g_scales[4 * c : P, v_cols],
+                        start=(c == 0 and d == 0),
+                        stop=(c == PASSES - 1 and d == D - 1),
+                    )
+
+        cast_x(0, 0)
+        cast_x(0, 1)
+        quantize_x(0, 0)
+        quantize_x(0, 1)
+        cast_x(1, 0)
+        gather_codes(0)
+        quantize_x(1, 0)
+        cast_x(1, 1)
+        quantize_x(1, 1)
+        cast_x(2, 0)
+        gather_codes(1)
+        cast_w(0, 0)
+        quantize_x(2, 0)
+        quantize_w(0, 0)
+        cast_x(2, 1)
+        quantize_x(2, 1)
+        gather_scales()
+        cast_w(0, 1)
+        quantize_w(0, 1)
+        multiply(0, 0)
+        multiply(0, 1)
+        gather_codes(2)
+        for c in (1, 2):
+            for d in range(D):
+                cast_w(c, d)
+                if W_SCALAR[c, d] == P:
+                    quantize_w(c, d, P, N)
+                    quantize_w(c, d, 0, P)
+                else:
+                    quantize_w(c, d)
+                multiply(c, d)
+
+        for m in range(M_TILES):
+            result = keep.tile([P, V], F32, name=f"result_{m}")
+            for i, (v0, v1) in enumerate(PIECES):
+                if m == 0:
+                    nc.scalar.activation(out=result[:, v0:v1], in_=acc[m, i][:], func=IDENTITY, bias=bias[:, m, :])
+                else:
+                    nc.vector.tensor_scalar(
+                        out=result[:, v0:v1], in0=acc[m, i][:], scalar1=bias[:, m, :], scalar2=None, op0=ADD
+                    )
+            queue = nc.scalar if m == 0 else nc.sync
+            queue.dma_start(out=out[m * P : (m + 1) * P, :], in_=result[:])

@@ -20,7 +20,7 @@ PACK = 4
 K_PASS = P * PACK
 PASSES = K // K_PASS
 HALF = 512
-X_SCALAR = {(0, 0): 176, (0, 1): 176, (1, 0): 384, (1, 1): 320, (2, 0): 352, (2, 1): 192}
+X_SCALAR = {(0, 0): 176, (0, 1): 176, (1, 0): 192, (1, 1): 336, (2, 0): 192, (2, 1): 304}
 W_SCALAR = {(0, 0): 256, (0, 1): 256, (1, 0): 256, (1, 1): 256, (2, 0): 256, (2, 1): 128}
 M_TILES = N // P
 PIECES = ((0, 256), (256, 384))
@@ -52,27 +52,25 @@ def tile_picked_merge_lin_bias_sub_e_kernel(tc, xT, w, b, offs, out):
         x_raw = {}
         w_raw = {}
 
-        def load_x(c, h):
-            x_raw[c, h] = keep.tile([P, PACK, HALF], F32, name=f"x_raw_{c}_{h}")
-            rows = xT[c * K_PASS : (c + 1) * K_PASS, h * HALF : (h + 1) * HALF]
-            nc.sync.dma_start(out=x_raw[c, h][:], in_=rows.rearrange("(p j) w -> p j w", j=PACK))
+        def load_x(c, t0, t1):
+            raw = keep.tile([P, PACK, t1 - t0], F32, name=f"x_raw_{c}_{t0}")
+            rows = xT[c * K_PASS : (c + 1) * K_PASS, t0:t1]
+            nc.sync.dma_start(out=raw[:], in_=rows.rearrange("(p j) w -> p j w", j=PACK))
+            for t in range(t0, t1, HALF):
+                x_raw[c, t // HALF] = raw[:, :, t - t0 : t - t0 + HALF]
 
         def load_w(c, d):
             w_raw[c, d] = keep.tile([P, PACK, N], F32, name=f"w_raw_{c}_{d}")
             rows = w[d, c * K_PASS : (c + 1) * K_PASS, :]
             nc.sync.dma_start(out=w_raw[c, d][:], in_=rows.rearrange("(p j) n -> p j n", j=PACK))
 
-        load_x(0, 0)
+        load_x(0, 0, HALF)
         nc.sync.dma_start(offsets[:], offs)
         nc.scalar.dma_start(out=bias[:], in_=b.rearrange("(c p) o -> p c o", p=P))
-        load_x(0, 1)
-        load_x(1, 0)
-        load_x(1, 1)
-        load_x(2, 0)
-        load_w(0, 0)
-        load_x(2, 1)
-        load_w(0, 1)
-        for c in (1, 2):
+        load_x(0, HALF, T)
+        load_x(1, 0, T)
+        load_x(2, 0, T)
+        for c in range(PASSES):
             for d in range(D):
                 load_w(c, d)
 
@@ -105,7 +103,7 @@ def tile_picked_merge_lin_bias_sub_e_kernel(tc, xT, w, b, offs, out):
             cast(x_bf[c, h], x_raw[c, h], X_SCALAR[c, h], HALF)
 
         def cast_w(c, d):
-            cast(w_bf[c, d], w_raw[c, d], W_SCALAR[c, d], N)
+            cast(w_bf[c, d], w_raw[c, d][:], W_SCALAR[c, d], N)
 
         def quantize_x(c, h):
             cols = slice(h * HALF, (h + 1) * HALF)
@@ -152,20 +150,20 @@ def tile_picked_merge_lin_bias_sub_e_kernel(tc, xT, w, b, offs, out):
         cast_x(0, 1)
         quantize_x(0, 0)
         quantize_x(0, 1)
-        cast_x(1, 0)
         gather_codes(0)
-        quantize_x(1, 0)
+        cast_x(1, 0)
         cast_x(1, 1)
+        quantize_x(1, 0)
         quantize_x(1, 1)
-        cast_x(2, 0)
         gather_codes(1)
-        cast_w(0, 0)
-        quantize_x(2, 0)
-        quantize_w(0, 0)
+        cast_x(2, 0)
         cast_x(2, 1)
+        quantize_x(2, 0)
         quantize_x(2, 1)
+        cast_w(0, 0)
         gather_scales()
         cast_w(0, 1)
+        quantize_w(0, 0)
         quantize_w(0, 1)
         multiply(0, 0)
         multiply(0, 1)

@@ -20,7 +20,7 @@ PACK = 4
 K_PASS = P * PACK
 PASSES = K // K_PASS
 HALF = 512
-X_SCALAR = {(0, 0): 176, (0, 1): 176, (1, 0): 192, (1, 1): 336, (2, 0): 192, (2, 1): 304}
+X_SCALAR = {(0, 0): 176, (0, 1): 176, (1, 0): 0, (1, 1): 448, (2, 0): 512, (2, 1): 208}
 W_SCALAR = {(0, 0): 256, (0, 1): 256, (1, 0): 256, (1, 1): 256, (2, 0): 256, (2, 1): 128}
 M_TILES = N // P
 PIECES = ((0, 256), (256, 384))
@@ -37,6 +37,7 @@ def tile_picked_merge_lin_bias_sub_e_kernel(tc, xT, w, b, offs, out):
     nc = tc.nc
     with ExitStack() as ctx:
         keep = ctx.enter_context(tc.tile_pool(name="keep", bufs=1))
+        gate = ctx.enter_context(tc.tile_pool(name="gate", bufs=1))
         psum = ctx.enter_context(tc.psum_pool(name="psum", bufs=1))
 
         offsets = keep.tile([P, S // 16], U16, name="offsets")
@@ -46,7 +47,7 @@ def tile_picked_merge_lin_bias_sub_e_kernel(tc, xT, w, b, offs, out):
         nc.gpsimd.memset(warm[:], 0.0)
         nc.scalar.activation(out=warmed[:], in_=warm[:], func=IDENTITY)
 
-        x_scales = keep.tile([P, T], U8, name="x_scales", align_bytes=64)
+        x_scales = gate.tile([P, T], U8, name="scales_then_w", align_bytes=64)
         nc.gpsimd.memset(x_scales[:], 0)
 
         x_raw = {}
@@ -69,7 +70,8 @@ def tile_picked_merge_lin_bias_sub_e_kernel(tc, xT, w, b, offs, out):
         nc.scalar.dma_start(out=bias[:], in_=b.rearrange("(c p) o -> p c o", p=P))
         load_x(0, HALF, T)
         load_x(1, 0, T)
-        load_x(2, 0, T)
+        load_x(2, 0, HALF)
+        load_x(2, HALF, T)
         for c in range(PASSES):
             for d in range(D):
                 load_w(c, d)
@@ -77,9 +79,10 @@ def tile_picked_merge_lin_bias_sub_e_kernel(tc, xT, w, b, offs, out):
         x_bf = {}
         for c in range(PASSES):
             for h in range(2):
-                x_bf[c, h] = keep.tile([P, HALF, PACK], BF16, name=f"x_bf_{c}_{h}", align_bytes=64)
-        x_codes = [keep.tile([P, T], U32, name=f"x_codes_{c}", align_bytes=64) for c in range(PASSES)]
-        g_codes = [keep.tile([P, S], U32, name=f"g_codes_{c}", align_bytes=64) for c in range(PASSES)]
+                if (c, h) != (2, 1):
+                    x_bf[c, h] = keep.tile([P, HALF, PACK], BF16, name=f"x_bf_{c}_{h}", align_bytes=64)
+        x_codes = [gate.tile([P, T], U32, name=f"codes_{c}", align_bytes=64) for c in range(2)]
+        g_codes = [keep.tile([P, S], U32, name=f"g_codes_{c}", align_bytes=64) for c in range(PASSES - 1)]
         g_scales = keep.tile([P, S], U8, name="g_scales", align_bytes=64)
 
         w_bf = {}
@@ -87,8 +90,12 @@ def tile_picked_merge_lin_bias_sub_e_kernel(tc, xT, w, b, offs, out):
         w_scales = {}
         for c in range(PASSES):
             for d in range(D):
-                w_bf[c, d] = keep.tile([P, N, PACK], BF16, name=f"w_bf_{c}_{d}", align_bytes=64)
-                w_codes[c, d] = keep.tile([P, N], U32, name=f"w_codes_{c}_{d}", align_bytes=64)
+                if (c, d) == (1, 1):
+                    w_bf[c, d] = gate.tile([P, N, PACK], BF16, name="gate", align_bytes=64)
+                elif (c, d) == (1, 0):
+                    w_bf[c, d] = gate.tile([P, N, PACK], BF16, name="w_then_codes", align_bytes=64)
+                else:
+                    w_bf[c, d] = keep.tile([P, N, PACK], BF16, name=f"w_bf_{c}_{d}", align_bytes=64)
                 w_scales[c, d] = keep.tile([P, N], U8, name=f"w_scales_{c}_{d}", align_bytes=64)
 
         def cast(dst, raw, cut, width):
@@ -105,13 +112,16 @@ def tile_picked_merge_lin_bias_sub_e_kernel(tc, xT, w, b, offs, out):
         def cast_w(c, d):
             cast(w_bf[c, d], w_raw[c, d][:], W_SCALAR[c, d], N)
 
-        def quantize_x(c, h):
-            cols = slice(h * HALF, (h + 1) * HALF)
+        def quantize_cols(c, t0, grouped):
+            cols = slice(t0, t0 + grouped.shape[1])
             nc.vector.quantize_mx(
                 out=x_codes[c][:, cols].bitcast(FP8X4),
                 scales=x_scales[4 * c : P, cols],
-                in_=x_bf[c, h][:].rearrange("p w j -> p (w j)"),
+                in_=grouped[:].rearrange("p w j -> p (w j)"),
             )
+
+        def quantize_x(c, h):
+            quantize_cols(c, h * HALF, x_bf[c, h])
 
         def gather_codes(c):
             nc.vector.tensor_copy(out=g_codes[c][:], in_=x_codes[c][:].indirect(offsets[:]))
@@ -155,37 +165,60 @@ def tile_picked_merge_lin_bias_sub_e_kernel(tc, xT, w, b, offs, out):
         cast_x(1, 1)
         quantize_x(1, 0)
         quantize_x(1, 1)
-        gather_codes(1)
         cast_x(2, 0)
-        cast_x(2, 1)
+        gather_codes(1)
+        x_codes.append(gate.tile([P, T], U32, name="codes_then_w", align_bytes=64))
+        quarter = HALF // 2
+        last_a = keep.tile([P, quarter, PACK], BF16, name="last_a", align_bytes=64)
+        last_b = gate.tile([P, quarter, PACK], BF16, name="codes_1", align_bytes=64)
+        cast(last_a, x_raw[2, 1][:, :, :quarter], quarter, quarter)
+        cast(last_b, x_raw[2, 1][:, :, quarter:], 0, quarter)
         quantize_x(2, 0)
-        quantize_x(2, 1)
+        quantize_cols(2, HALF + quarter, last_b)
+        quantize_cols(2, HALF, last_a)
         cast_w(0, 0)
-        gather_scales()
         cast_w(0, 1)
+        gather_scales()
+        w_early = gate.tile([P, 2 * D * N], U32, name="scales_then_w", align_bytes=64)
+        w_late = keep.tile([P, D * N], U32, name="w_late", align_bytes=64)
+        for d in range(D):
+            w_codes[0, d] = w_early[:, d * N : (d + 1) * N]
+            w_codes[1, d] = w_early[:, (D + d) * N : (D + d + 1) * N]
+            w_codes[2, d] = w_late[:, d * N : (d + 1) * N]
         quantize_w(0, 0)
         quantize_w(0, 1)
         multiply(0, 0)
         multiply(0, 1)
+        cast_w(1, 0)
+        quantize_w(1, 0)
+        multiply(1, 0)
+        g_codes.append(gate.tile([P, S], U32, name="w_then_codes", align_bytes=64))
         gather_codes(2)
-        for c in (1, 2):
-            for d in range(D):
-                cast_w(c, d)
-                if W_SCALAR[c, d] == P:
-                    quantize_w(c, d, P, N)
-                    quantize_w(c, d, 0, P)
-                else:
-                    quantize_w(c, d)
-                multiply(c, d)
+        cast_w(1, 1)
+        quantize_w(1, 1)
+        multiply(1, 1)
+        cast_w(2, 0)
+        quantize_w(2, 0)
+        multiply(2, 0)
+        tail = gate.tile([P, P, PACK], BF16, name="gate", align_bytes=64)
+        cast(tail, w_raw[2, 1][:, :, P:], 0, P)
+        cast(w_bf[2, 1], w_raw[2, 1][:, :, :P], P, P)
+        nc.vector.quantize_mx(
+            out=w_codes[2, 1][:, P:N].bitcast(FP8X4),
+            scales=w_scales[2, 1][:, P:N],
+            in_=tail[:].rearrange("p n j -> p (n j)"),
+        )
+        quantize_w(2, 1, 0, P)
+        multiply(2, 1)
 
-        for m in range(M_TILES):
+        for m in (1, 0):
             result = keep.tile([P, V], F32, name=f"result_{m}")
             for i, (v0, v1) in enumerate(PIECES):
-                if m == 0:
+                if m == 1:
                     nc.scalar.activation(out=result[:, v0:v1], in_=acc[m, i][:], func=IDENTITY, bias=bias[:, m, :])
                 else:
                     nc.vector.tensor_scalar(
                         out=result[:, v0:v1], in0=acc[m, i][:], scalar1=bias[:, m, :], scalar2=None, op0=ADD
                     )
-            queue = nc.scalar if m == 0 else nc.sync
+            queue = nc.scalar if m == 1 else nc.sync
             queue.dma_start(out=out[m * P : (m + 1) * P, :], in_=result[:])

from contextlib import ExitStack

import concourse.mybir as mybir

K, T, D, S, V, N = 1536, 1024, 2, 768, 384, 256
FLOPS = 2 * N * V * D * K

F32 = mybir.dt.float32
BF16 = mybir.dt.bfloat16
U32 = mybir.dt.uint32
U16 = mybir.dt.uint16
U8 = mybir.dt.uint8
FP8X4 = mybir.dt.float8_e4m3fn_x4
COPY = mybir.ActivationFunctionType.Copy
IDENTITY = mybir.ActivationFunctionType.Identity
ADD = mybir.AluOpType.add

P = 128
PACK = 4
K_PASS = P * PACK
PASSES = K // K_PASS
HALF = 512
X_SCALAR = {(0, 0): 176, (0, 1): 176, (1, 0): 0, (1, 1): 448, (2, 0): 512, (2, 1): 208}
W_SCALAR = {(0, 0): 256, (0, 1): 256, (1, 0): 256, (1, 1): 256, (2, 0): 256, (2, 1): 128}
M_TILES = N // P
PIECES = ((0, 256), (256, 384))


def regroup(dst, raw):
    return (
        dst.rearrange("p (c i) t -> p c t i", i=4),
        raw.rearrange("p t (c i) -> p c t i", i=4),
    )


def tile_picked_merge_lin_bias_sub_e_kernel(tc, xT, w, b, offs, out):
    nc = tc.nc
    with ExitStack() as ctx:
        keep = ctx.enter_context(tc.tile_pool(name="keep", bufs=1))
        gate = ctx.enter_context(tc.tile_pool(name="gate", bufs=1))
        psum = ctx.enter_context(tc.psum_pool(name="psum", bufs=1))

        offsets = keep.tile([P, S // 16], U16, name="offsets")
        bias = keep.tile([P, M_TILES, 1], F32, name="bias")
        warm = keep.tile([P, 1], F32, name="warm")
        warmed = keep.tile([P, 1], F32, name="warmed")
        nc.gpsimd.memset(warm[:], 0.0)
        nc.scalar.activation(out=warmed[:], in_=warm[:], func=IDENTITY)

        x_scales = gate.tile([P, T], U8, name="scales_then_w", align_bytes=64)
        nc.gpsimd.memset(x_scales[:], 0)

        x_raw = {}
        w_raw = {}

        def load_x(c, t0, t1):
            raw = keep.tile([P, PACK, t1 - t0], F32, name=f"x_raw_{c}_{t0}")
            rows = xT[c * K_PASS : (c + 1) * K_PASS, t0:t1]
            nc.sync.dma_start(out=raw[:], in_=rows.rearrange("(p j) w -> p j w", j=PACK))
            for t in range(t0, t1, HALF):
                x_raw[c, t // HALF] = raw[:, :, t - t0 : t - t0 + HALF]

        def load_w(c, d):
            w_raw[c, d] = keep.tile([P, PACK, N], F32, name=f"w_raw_{c}_{d}")
            rows = w[d, c * K_PASS : (c + 1) * K_PASS, :]
            nc.sync.dma_start(out=w_raw[c, d][:], in_=rows.rearrange("(p j) n -> p j n", j=PACK))

        load_x(0, 0, HALF)
        nc.sync.dma_start(offsets[:], offs)
        nc.scalar.dma_start(out=bias[:], in_=b.rearrange("(c p) o -> p c o", p=P))
        load_x(0, HALF, T)
        load_x(1, 0, T)
        load_x(2, 0, HALF)
        load_x(2, HALF, T)
        for c in range(PASSES):
            for d in range(D):
                load_w(c, d)

        x_bf = {}
        for c in range(PASSES):
            for h in range(2):
                if (c, h) != (2, 1):
                    x_bf[c, h] = keep.tile([P, HALF, PACK], BF16, name=f"x_bf_{c}_{h}", align_bytes=64)
        x_codes = [gate.tile([P, T], U32, name=f"codes_{c}", align_bytes=64) for c in range(2)]
        g_codes = [keep.tile([P, S], U32, name=f"g_codes_{c}", align_bytes=64) for c in range(PASSES - 1)]
        g_scales = keep.tile([P, S], U8, name="g_scales", align_bytes=64)

        w_bf = {}
        w_codes = {}
        w_scales = {}
        for c in range(PASSES):
            for d in range(D):
                if (c, d) == (1, 1):
                    w_bf[c, d] = gate.tile([P, N, PACK], BF16, name="gate", align_bytes=64)
                elif (c, d) == (1, 0):
                    w_bf[c, d] = gate.tile([P, N, PACK], BF16, name="w_then_codes", align_bytes=64)
                else:
                    w_bf[c, d] = keep.tile([P, N, PACK], BF16, name=f"w_bf_{c}_{d}", align_bytes=64)
                w_scales[c, d] = keep.tile([P, N], U8, name=f"w_scales_{c}_{d}", align_bytes=64)

        def cast(dst, raw, cut, width):
            if cut > 0:
                out_view, in_view = regroup(dst[:, :cut, :], raw[:, :, :cut])
                nc.scalar.activation(out=out_view, in_=in_view, func=COPY)
            if cut < width:
                out_view, in_view = regroup(dst[:, cut:, :], raw[:, :, cut:])
                nc.vector.tensor_copy(out=out_view, in_=in_view)

        def cast_x(c, h):
            cast(x_bf[c, h], x_raw[c, h], X_SCALAR[c, h], HALF)

        def cast_w(c, d):
            cast(w_bf[c, d], w_raw[c, d][:], W_SCALAR[c, d], N)

        def quantize_cols(c, t0, grouped):
            cols = slice(t0, t0 + grouped.shape[1])
            nc.vector.quantize_mx(
                out=x_codes[c][:, cols].bitcast(FP8X4),
                scales=x_scales[4 * c : P, cols],
                in_=grouped[:].rearrange("p w j -> p (w j)"),
            )

        def quantize_x(c, h):
            quantize_cols(c, h * HALF, x_bf[c, h])

        def gather_codes(c):
            nc.vector.tensor_copy(out=g_codes[c][:], in_=x_codes[c][:].indirect(offsets[:]))

        def quantize_w(c, d, m0=0, m1=N):
            nc.vector.quantize_mx(
                out=w_codes[c, d][:, m0:m1].bitcast(FP8X4),
                scales=w_scales[c, d][:, m0:m1],
                in_=w_bf[c, d][:, m0:m1, :].rearrange("p n j -> p (n j)"),
            )

        def gather_scales():
            nc.vector.tensor_copy(out=g_scales[:], in_=x_scales[:].indirect(offsets[:]))

        acc = {}
        for m in range(M_TILES):
            for i, (v0, v1) in enumerate(PIECES):
                acc[m, i] = psum.tile([P, v1 - v0], F32, name=f"acc_{m}_{i}")

        def multiply(c, d):
            for m in (1, 0):
                m_cols = slice(m * P, (m + 1) * P)
                for i, (v0, v1) in enumerate(PIECES):
                    v_cols = slice(d * V + v0, d * V + v1)
                    nc.tensor.matmul_mx(
                        out=acc[m, i][:],
                        lhsT=w_codes[c, d][:, m_cols].bitcast(FP8X4),
                        lhsT_scale=w_scales[c, d][:, m_cols],
                        rhs=g_codes[c][:, v_cols].bitcast(FP8X4),
                        rhs_scale=g_scales[4 * c : P, v_cols],
                        start=(c == 0 and d == 0),
                        stop=(c == PASSES - 1 and d == D - 1),
                    )

        cast_x(0, 0)
        cast_x(0, 1)
        quantize_x(0, 0)
        quantize_x(0, 1)
        gather_codes(0)
        cast_x(1, 0)
        cast_x(1, 1)
        quantize_x(1, 0)
        quantize_x(1, 1)
        cast_x(2, 0)
        gather_codes(1)
        x_codes.append(gate.tile([P, T], U32, name="codes_then_w", align_bytes=64))
        quarter = HALF // 2
        last_a = keep.tile([P, quarter, PACK], BF16, name="last_a", align_bytes=64)
        last_b = gate.tile([P, quarter, PACK], BF16, name="codes_1", align_bytes=64)
        cast(last_a, x_raw[2, 1][:, :, :quarter], quarter, quarter)
        cast(last_b, x_raw[2, 1][:, :, quarter:], 0, quarter)
        quantize_x(2, 0)
        quantize_cols(2, HALF + quarter, last_b)
        quantize_cols(2, HALF, last_a)
        cast_w(0, 0)
        cast_w(0, 1)
        gather_scales()
        w_early = gate.tile([P, 2 * D * N], U32, name="scales_then_w", align_bytes=64)
        w_late = keep.tile([P, D * N], U32, name="w_late", align_bytes=64)
        for d in range(D):
            w_codes[0, d] = w_early[:, d * N : (d + 1) * N]
            w_codes[1, d] = w_early[:, (D + d) * N : (D + d + 1) * N]
            w_codes[2, d] = w_late[:, d * N : (d + 1) * N]
        quantize_w(0, 0)
        quantize_w(0, 1)
        multiply(0, 0)
        multiply(0, 1)
        cast_w(1, 0)
        quantize_w(1, 0)
        multiply(1, 0)
        g_codes.append(gate.tile([P, S], U32, name="w_then_codes", align_bytes=64))
        gather_codes(2)
        cast_w(1, 1)
        quantize_w(1, 1)
        multiply(1, 1)
        cast_w(2, 0)
        quantize_w(2, 0)
        multiply(2, 0)
        tail = gate.tile([P, P, PACK], BF16, name="gate", align_bytes=64)
        cast(tail, w_raw[2, 1][:, :, P:], 0, P)
        cast(w_bf[2, 1], w_raw[2, 1][:, :, :P], P, P)
        nc.vector.quantize_mx(
            out=w_codes[2, 1][:, P:N].bitcast(FP8X4),
            scales=w_scales[2, 1][:, P:N],
            in_=tail[:].rearrange("p n j -> p (n j)"),
        )
        quantize_w(2, 1, 0, P)
        multiply(2, 1)

        for m in (1, 0):
            result = keep.tile([P, V], F32, name=f"result_{m}")
            for i, (v0, v1) in enumerate(PIECES):
                if m == 1:
                    nc.scalar.activation(out=result[:, v0:v1], in_=acc[m, i][:], func=IDENTITY, bias=bias[:, m, :])
                else:
                    nc.vector.tensor_scalar(
                        out=result[:, v0:v1], in0=acc[m, i][:], scalar1=bias[:, m, :], scalar2=None, op0=ADD
                    )
            queue = nc.scalar if m == 1 else nc.sync
            queue.dma_start(out=out[m * P : (m + 1) * P, :], in_=result[:])
